import numpy as np, ml_dtypes
CORES = [36,164,52,180,100,228,116,244]
N = 8
BF = ml_dtypes.bfloat16
def gentries(a):
    return np.ascontiguousarray(a.reshape(8, 16, -1).transpose(0, 2, 1)).reshape(8, -1)
def gtable(e):
    e = np.asarray(e); return np.ascontiguousarray(e.reshape(8, -1, 16).transpose(0, 2, 1)).reshape(128, -1).astype(np.int32)
V, B, K, PH, CAP, R, ZP, M = 512, 256, 16, 2, 16, 4, 1024, 256
NC, TH = N * CAP, 2047
def parts(rng):
    c = rng.integers(0, 256, (N, 8, 16, V)); low = rng.random((N, 8, 1, V)) < 0.125; c = np.where(low, rng.integers(0, 41, c.shape), c)
    z = rng.integers(0, 256, (N, 8, 16, ZP)); hi = np.argsort(rng.random((N, 8, ZP)), axis=-1)[..., :ZP // 4]
    mark = np.zeros((N, 8, ZP), bool); np.put_along_axis(mark, hi, True, 2); z = np.where(mark[:, :, None], rng.integers(200, 256, z.shape), z)
    e = rng.integers(0, ZP, (N, 8, K, V)); far = np.take_along_axis(hi, rng.integers(0, ZP // 4, (N, 8, K * V)), 2).reshape(N, 8, K, V)
    e = np.where(low & (rng.random((N, 8, 1, V)) < 0.5), far, e)
    p = np.argsort(rng.random((8, K, N * V)), axis=-1)
    share = rng.choice(np.array([0.3, 0.5, 0.75, 1.0]), (N, 8, 1, 1))
    j = np.where(rng.random((N, 8, 1, M)) < share, rng.integers(0, 256, (N, 8, 16, M)), rng.integers(0, 7, (N, 8, 16, M)))
    x = np.clip(c + rng.integers(-6, 7, c.shape), 0, 255)
    return c, z, e, p, j, x
def order(a):
    s = a.shape[:-2]; return np.ascontiguousarray(np.swapaxes(a.reshape(s + (K, PH, B)), -3, -2)).reshape(s + (K * V,))
def small(a):
    return np.ascontiguousarray(a.reshape(N, 128, -1)).astype(np.float32).astype(BF)
def pack(c, z, e, p, j, x):
    n = order(np.ascontiguousarray(p.reshape(8, K, N, V).transpose(2, 0, 1, 3)))
    return {"cen": small(c), "pl": small(z), "ent": order(e).astype(np.int32), "nb": np.stack([gtable(a) for a in n]), "jmp": small(j), "wk": small(x)}
def even(c, j):
    c[:, :, 0] = c[:, :, 0] ^ (np.add.reduce(c, axis=2) & 1); j[..., 0::2] = 0
def steer(rng, c, p, x, cnt, face, last=None):
    x[..., :B] = c[..., :B]
    for g in range(8):
        al = c[:, g].transpose(1, 0, 2).reshape(16, N * V); P = np.full(N * V, -1); pos = {}
        for q in range(N):
            i = rng.permutation(B); at = 0
            if last is not None and last[g, q] >= 0:
                m = int(np.add.reduce(cnt[g, q, :int(last[g, q]) + 1])) - 1; i[i == B - 1] = i[m]; i[m] = B - 1
            for o in range(N):
                n = int(cnt[g, q, o]); pos[q, o] = q * V + i[at:at + n]; at += n
            s = pos[q, q]
            if len(s): P[s] = np.roll(s, 1) if len(s) > 1 else q * V + (s - q * V + 1) % V
        for o in range(N):
            left = rng.permutation(np.setdiff1d(np.arange(o * V, (o + 1) * V), P)); at = 0
            for q in range(N):
                if q != o:
                    s = pos[q, o]; P[s] = left[at:at + len(s)]; at += len(s)
        go = np.nonzero(P >= 0)[0]; r = go // V
        x[r, g, :, go - r * V] = al[:, P[go]].T
        P[P < 0] = rng.permutation(np.setdiff1d(np.arange(N * V), P)); p[g, face[g]] = P
def plant(P, at, val):
    i = int(np.argmax(P == val)); P[i] = P[at]; P[at] = val
def setup_inputs(rng):
    return pack(*parts(rng))
def setup_inputs_corners(rng):
    c, z, e, p, j, x = parts(rng); even(c, j); cnt = np.zeros((8, N, N), np.int64); many = B // 2
    face = rng.integers(0, K, 8); face[0] = K - 1; face[7] = 0
    for g in range(8):
        room = [V] * N
        for q in range(N):
            left = B
            for h in [1] + [int(a) for a in rng.permutation(N) if a != 1]:
                o = (q + h) % N; n = int(rng.choice(np.array([0, 1, CAP - 1, CAP, CAP + 1, many])))
                if q == 0 and h == 1: n = (CAP, CAP + 1, many, CAP - 1, 1, 0, CAP, CAP)[g]
                n = min(n, left, room[o]); cnt[g, q, o] = n; left -= n; room[o] -= n
    steer(rng, c, p, x, cnt, face)
    for g in (1, 5): p[g, (face[g] + 1) % K] = np.arange(N * V)
    m = rng.random((N, 4, 1, V)) < 0.5
    e[:, ::2] = np.where(m, rng.choice(np.array([0, NC - 1, NC, R * NC - 1, R * NC, ZP - 1]), (N, 4, K, V)), e[:, ::2])
    return pack(c, z, e, p, j, x)
def setup_inputs_crowd(rng):
    c, z, e, p, j, x = parts(rng); even(c, j); cnt = np.zeros((8, N, N), np.int64); face = rng.integers(0, K, 8); last = np.full((8, N), -1)
    for g in range(8):
        for q in range(N):
            n = int(rng.choice(np.array([B, B - 1, B // 2, 0])))
            if q == 0: n = B
            if q == 1: n = B - 1 if g == 0 else B
            if q == 2 and g % 2 == 1: n = min(n, B // 2)
            cnt[g, q, (q + g) % N] = n
        if g % 2 == 1:
            n = int(rng.choice(np.array([1, CAP]))); o = (g + 2) % N
            if g == 7: n = CAP
            cnt[g, 0, g % N] -= n; cnt[g, 0, o] += n; last[g, 0] = o
    steer(rng, c, p, x, cnt, face, last)
    return pack(c, z, e, p, j, x)
def setup_inputs_ties(rng):
    c, z, e, p, j, x = parts(rng)
    c = rng.integers(0, 9, c.shape); z = rng.integers(0, 9, z.shape); j = rng.integers(0, 9, j.shape); x = rng.integers(0, 9, x.shape)
    c[:, ::2, :, 1::2] = c[:, ::2, :, 0::2]
    z[:, 3] = rng.integers(128, 136, z[:, 3].shape); z[:, 5] = rng.integers(248, 256, z[:, 5].shape)
    e = np.where(rng.random((N, 8, 1, V)) < 0.6, rng.integers(0, ZP, (N, 8, 1, V)), rng.integers(0, ZP, (N, 8, K, V)))
    i = np.concatenate([np.array([0, B - 1]), 1 + rng.permutation(B - 2)[:6]])
    c[..., i] = 8; x[..., i] = 2; j[..., 0] = 0; z[..., ZP - 2:] = 8; z[:, :, 15, ZP - 2] = 7
    e[:, :, :K // 2, i] = ZP - 1; e[:, :, K // 2:, i] = ZP - 2
    return pack(c, z, e, p, j, x)
def setup_inputs_spread(rng):
    c, z, e, p, j, x = parts(rng)
    c, z, j, x = [(np.exp2(8 * rng.random((N, 8, 1, n))) * rng.random((N, 8, 16, n))).astype(np.int64) for n in (V, ZP, M, V)]
    e = np.minimum((ZP * rng.random(e.shape) ** 3).astype(np.int64), ZP - 1)
    return pack(c, z, e, p, j, x)
def setup_inputs_ends(rng):
    p = np.argsort(rng.random((8, K, N * V)), axis=-1)
    c, z, j, x = [255 * (rng.random((N, 8, 16, n)) < rng.choice(np.array([0.0, 0.1, 0.5, 0.9, 1.0]), (N, 8, 1, n))).astype(np.int64) for n in (V, ZP, M, V)]
    e = (ZP - 1) * rng.integers(0, 2, (N, 8, K, V))
    z[..., 0] = 255; z[..., ZP - 1] = 0; j[..., 65280 & (M - 1)] = 0
    for a, b in ((0, 1), (V - 1, V - 2)):
        c[..., a] = 0; c[..., b] = 255; x[..., a] = 255; e[..., a] = ZP - 1
    for a in (2, B - 3):
        c[..., a] = 0; x[..., a] = 255
    for g in range(8):
        for k in range(K):
            for a in range(N):
                o = ((a + 1) % N) * V; near = (g + k) % 2 == 0
                plant(p[g, k], a * V, o + (1 if near else 0)); plant(p[g, k], a * V + V - 1, o + (V - 2 if near else V - 1))
                plant(p[g, k], a * V + 2, o + 2); plant(p[g, k], a * V + B - 3, o + B - 3)
    u = rng.random((N, 1, V)); nz = np.where(u < 0.5, 8, np.where(u < 0.95, 7, 0))
    c[:, 6] = np.where(np.arange(16)[None, :, None] < nz, 0, 255); z[:, 6] = 255; x[:, 6] = 255; j[:, 6] = 0; e[:, 6] = ZP - 1
    return pack(c, z, e, p, j, x)
def check_inputs(d):
    bad = []
    for k, hi in (("cen", 255), ("pl", 255), ("jmp", 255), ("wk", 255), ("ent", ZP - 1), ("nb", N * V - 1)):
        v = np.asarray(d[k]).astype(np.float32)
        if not np.all((v >= 0) & (v <= hi) & (v == np.floor(v))): bad.append("range of " + k)
    a = np.stack([gentries(q) for q in d["nb"]]).reshape(N, 8, PH, K, B).transpose(1, 3, 0, 2, 4).reshape(8, K, N * V)
    if np.any(np.sort(a, axis=-1) != np.arange(N * V)): bad.append("neighbours k of all boxes all different")
    return bad
def reference(cen, pl, ent, nb, jmp, wk):
    C, Z, D, X = [a.astype(np.float32).astype(np.int32).reshape(N, 8, 16, -1) for a in (cen, pl, jmp, wk)]
    E = ent.astype(np.int32).reshape(N, 8, PH, K, B); F = np.ones((N, 8, PH, K, B), np.int32)
    L = np.stack([gentries(a) for a in nb]).reshape(N, 8, PH, K, B); A = [0] * N
    w = (2 * np.arange(16, dtype=np.int32) + 1)[None, None, :, None]
    for t in range(R):
        b = t % PH; lo, hi = b * B, b * B + B
        x = X[..., lo:hi]; ix = np.add.reduce(w * x, axis=2) & (M - 1)
        y = np.abs(x - np.take_along_axis(D, ix[:, :, None, :], 3))
        al = np.ascontiguousarray(C.transpose(1, 2, 0, 3)).reshape(8, 16, N * V)
        outs = []
        for q in range(N):
            c = C[q, :, :, lo:hi].astype(np.int32); yq = y[q]; n = L[q, :, b]
            v = np.take_along_axis(al, n.reshape(8, 1, K * B), 2).reshape(8, 16, K, B)
            d = np.add.reduce(np.abs(v - yq[:, :, None, :]), axis=1)
            k = np.argmin(d, axis=1); own = np.add.reduce(np.abs(c - yq), axis=1)
            go = np.min(d, axis=1) + (A[q] & 63) < own
            s = np.take_along_axis(Z[q], E[q, :, b].reshape(8, 1, K * B), 2).reshape(8, 16, K, B)
            h = np.add.reduce(np.abs(s - c[:, :, None, :]), axis=1)
            P = np.add.accumulate(F[q, :, b] * np.maximum(TH - h, 0), axis=1)
            u = np.add.reduce(yq, axis=1) & 63
            ok = 64 * P > (u * P[:, K - 1])[:, None, :]
            first = np.argmax(ok, axis=1)
            z = np.take_along_axis(s, first[:, None, None, :], 2)[:, :, 0]
            z = np.where(np.any(ok, axis=1)[:, None, :], z, c)
            new = np.where(go[:, None, :], z, yq)
            X[q, :, :, lo:hi] = new; C[q, :, :, lo:hi] = c + np.clip(new - c, -1, 1)
            A[q] = int(np.count_nonzero(go))
            outs.append((go, np.take_along_axis(n, k[:, None, :], 1)[:, 0], k))
        land = np.zeros((N, 8, 16, NC), np.int32)
        for q in range(N):
            go, to, k = outs[q]
            for o in range(N):
                hit = go & (to // V == o); at = np.add.accumulate(hit.astype(np.int64), axis=1) - 1
                g, i = np.nonzero(hit & (at < CAP)); s = q * CAP + at[g, i]
                land[o][g, :, s] = y[q][g, :, i]
                v = to[g, i] - o * V; bl = v // B; row = k[g, i] ^ 1
                E[o][g, bl, row, v - bl * B] = NC * t + s
                F[o][g, bl, row, v - bl * B] += 1
        Z[..., NC * t:NC * t + NC] = land
    return {"yc": C.reshape(N, 128, V).astype(np.float32).astype(BF), "yx": X.reshape(N, 128, V).astype(np.float32).astype(BF), "yz": Z.reshape(N, 128, ZP).astype(np.float32).astype(BF),
            "ye": E.reshape(N, 8, K * V).astype(np.float32), "yn": F.reshape(N, 8, K * V).astype(np.float32).astype(BF)}

from concourse.bass import DstId, RemoteDMATransfer
from concourse.mybir import AluOpType as A, ActivationFunctionType as F

N, B, R = 8, 256, 4
YO = 8192
HELP = (2, 2)
VG = (2, 2, 2, 2)
HCH = ((0, 128, 256), (0, 128, 192, 256))
RECV_AT = 0
LIST_AT = 2
TAIL = 1
HV = (0, 0, 0, 0)
bf, f32, i32, u16 = "bfloat16", "float32", "int32", "uint16"
RELAY = ("tb",)


def _sb(n, d):
    return ("sbuf", [128, n], d)


SCRATCH = {
    "tb": _sb(5 * 2048, bf), "cf": _sb(256, bf), "xw": _sb(512, bf), "jm": _sb(256, bf), "pool": _sb(1536, bf),
    "sb": _sb(YO + 256, bf), "me": _sb(4096, bf), "ng": _sb(4096, bf), "mn": _sb(4096, bf),
    "mb": _sb(8336, f32), "m2": _sb(512, f32), "e2": _sb(512, i32), "nbi": _sb(512, i32),
    "outw": _sb(2304, f32), "land": _sb(512, f32), "n2": _sb(512, bf), "nt": _sb(512, bf), "ef": _sb(512, f32),
    "ti": _sb(256, i32), "ti2": _sb(256, i32), "ti3": _sb(256, i32), "ib": _sb(256, bf), "bk": _sb(256, bf),
    "town": _sb(544, bf), "tcode": _sb(544, f32), "nl": _sb(512, u16), "el": _sb(256, u16),
    "iot": _sb(256, bf), "x2": _sb(128, bf), "x3": _sb(256, bf), "kx": _sb(256, bf), "pi": _sb(8, i32), "pj": _sb(8, i32),
    "cc": _sb(64, f32), "bz": _sb(6 * 144, bf), "idn": _sb(6 * 128, bf), "id32": _sb(128, f32), "bo": _sb(128, bf), "bo32": _sb(128, f32),
    "tr0": _sb(128, f32), "tri": _sb(128, f32), "aw": _sb(128, bf), "dg": _sb(256, bf), "d0": _sb(128, f32), "d1": _sb(128, f32),
    "plc": _sb(512, f32), "dum": _sb(16, f32), "yoff": _sb(16, f32), "zb": _sb(16, bf),
    "s1": _sb(16, i32), "s2": _sb(16, i32), "jl": _sb(16, u16), "dy": _sb(256, bf), "da": _sb(256, bf),
    "ui": _sb(256, i32), "uu": _sb(256, i32), "cm": _sb(256, bf), "sk": _sb(16, f32), "sa": _sb(4, f32),
    "a1": _sb(4, i32), "a2": _sb(4, i32), "gk": _sb(256, f32), "up": _sb(256, f32), "no": _sb(256, bf), "zo": _sb(16, f32),
    "k0": _sb(64, f32), "k1": _sb(64, f32), "k2": _sb(32, f32), "ki": _sb(16, i32), "lo": _sb(16, i32), "l1": _sb(16, u16),
    "mo": _sb(256, bf), "mc": _sb(256, f32), "hit": _sb(256, bf), "cum": _sb(256, bf), "val": _sb(256, bf), "pay": _sb(256, f32),
    "dl": _sb(16, u16), "t1": _sb(16, f32), "t2": _sb(16, f32), "t3": _sb(16, f32), "l2": _sb(16, u16), "c1": _sb(256, bf),
    "yi": _sb(128, i32), "fr": _sb(128, f32), "sc": _sb(128, f32), "rl": _sb(8, u16), "fl": _sb(512, bf), "sg": _sb(512, bf),
}
for _j in range(8):
    SCRATCH["p%d" % _j] = ("psum", [128, 512], f32)
NDMA = 70
SEMAPHORES = (["qv", "qs", "qt", "qg"] + ["d%d" % j for j in range(NDMA)] + ["ax%d" % t for t in range(R)] + ["lx%d" % t for t in range(R)]
              + ["ac%d" % t for t in range(R + 1)] + ["lc%d" % t for t in range(R + 1)])


def helpers(T, topo, q):
    c = T.cores[q]
    can = [h for h in topo.cores_of(c) if h != c and all(topo.may_write(h, o) for o in T.cores)]
    far = [h for h in can if topo.die(h) != topo.die(c)]
    near = [h for h in can if topo.die(h) == topo.die(c)]
    return far[:HELP[0]] + near[:HELP[1]]


def shares(n, parts):
    out = [1] * parts
    j = 0
    while sum(out) + out[j % parts] <= n:
        out[j % parts] *= 2
        j += 1
    return out


def transfers(topo, core, engines, dsts, sem, srcs, dst):
    trs, at = [], 0
    for d, n, s in zip(dsts, shares(len(engines), len(dsts)), srcs):
        rid, pid = topo.addr(d, core)
        trs.append(RemoteDMATransfer(dst_ids=[DstId(rid=rid, pnc=pid)], dma_engine_mask=sum(1 << e for e in engines[at:at + n]),
                                     remote_sem=sem, src=s, dst=dst))
        at += n
    return trs, at


def centre_plan(T, topo, q):
    c, hs = T.cores[q], helpers(T, topo, q)
    peers = [(q + d) % N for d in range(1, N)]
    nd = max(0, N - 1 - 2 * len(hs))
    plan = {c: peers[:nd]}
    for j, h in enumerate(hs):
        plan[h] = peers[nd + 2 * j:nd + 2 * j + 2]
    off = topo.engines(c, T.cores[peers[0]])
    inner = [e for e in topo.engines(c, hs[0]) if nd == 0 or e not in off] if hs else []
    return plan, off, inner


def helper_program(g, core, T, topo, q):
    plan, off, inner = centre_plan(T, topo, q)
    hs = helpers(T, topo, q)
    got = shares(len(inner), len(hs))[hs.index(core)]
    dsts = [T.cores[o] for o in plan[core]]
    used = 0
    for reg in range(R + 1):
        slot = T.tb[:, 2048 * reg + B * q:2048 * reg + B * q + B]
        g.wait_ge(T.sem["ac%d" % reg], got)
        trs, used = transfers(topo, core, topo.engines(core, dsts[0]), dsts, T.sem["ac%d" % reg], [slot] * len(dsts), slot)
        g.remote_dma_fused(trs, local_sem=T.sem["lc%d" % reg])
    for reg in range(R + 1):
        g.wait_ge(T.sem["lc%d" % reg], used)


def rank_program(g, core, T, topo):
    me = T.rank_of(core)
    if me is None:
        for q in range(N):
            if core in helpers(T, topo, q):
                helper_program(g, core, T, topo, q)
        return
    eng = {"v": g.vector, "s": g.scalar, "t": g.tensor, "g": g, "y": g.sync}
    count = {"v": 0, "s": 0, "t": 0, "g": 0}
    known = {q: {} for q in eng}
    acc = {}
    final = {}
    ndma = [0]

    def order(q, reads, writes):
        need = {}
        for rg, w in ((reads, False), (writes, True)):
            for name, lo, hi in rg:
                ps = SCRATCH[name][0] == "psum"
                for a in acc.get(name, []):
                    if ps:
                        if a[3] == q and (q == "t" or not (w or a[2]) or a[1] <= lo or hi <= a[0]):
                            continue
                    elif a[1] <= lo or hi <= a[0] or not (w or a[2]) or (q == "t" and a[3] == "t"):
                        continue
                    sem, val, clock = a[4]
                    if need.get(sem, (0, None))[0] < val:
                        need[sem] = (val, clock)
        for sem, (val, clock) in sorted(need.items(), key=lambda e: -len(e[1][1])):
            if known[q].get(sem, 0) < val:
                eng[q].wait_ge(T.sem[sem], val)
                known[q][sem] = val
                for s2, v2 in clock.items():
                    if known[q].get(s2, 0) < v2:
                        known[q][s2] = v2

    def note(q, reads, writes, ev):
        for rg, w in ((reads, False), (writes, True)):
            for name, lo, hi in rg:
                old = acc.get(name, [])
                if w:
                    old = [a for a in old if not (lo <= a[0] and a[1] <= hi)]
                else:
                    old = [a for a in old if not (a[3] == q and not a[2] and lo <= a[0] and a[1] <= hi and a[4][0] == ev[0])]
                acc[name] = old + [[lo, hi, w, q, ev]]
        final[ev[0]] = max(final.get(ev[0], 0), ev[1])

    def regs(xs):
        out = []
        for x in xs:
            if isinstance(x, tuple):
                out += x[1]
        return out

    def ap(x):
        return x[0] if isinstance(x, tuple) else x

    def op(q, outs, ins, call):
        rd, wr = regs(ins), regs(outs)
        order(q, rd, wr)
        count[q] += 1
        call().then_inc(T.sem["q" + q], 1)
        note(q, rd, wr, ("q" + q, count[q], dict(known[q])))

    def v(name, lo=0, hi=None, step=1):
        if hi is None:
            hi = SCRATCH[name][1][1]
        return (T[name][:, lo:hi] if step == 1 else T[name][:, lo:hi:step], [(name, lo, hi)])

    def ind(win, off):
        return (win[0].indirect(off[0]), win[1] + off[1])

    def iout(win, off):
        return (win[0].indirect(off[0]), win[1]), off

    def dma(q, out, in_):
        rd, wr = regs([in_]), regs([out])
        order(q, rd, wr)
        sem = "d%d" % ndma[0]
        ndma[0] += 1
        eng[q].dma_start(ap(out), ap(in_)).then_inc(T.sem[sem], 16)
        note("d", rd, wr, (sem, 16, dict(known[q])))

    def cp(out, in_, extra=None):
        op("v", [out], [in_, extra], lambda: g.vector.tensor_copy(out[0], in_[0]))

    def tt(out, a, b, o):
        op("v", [out], [a, b], lambda: g.vector.tensor_tensor(out[0], a[0], b[0], o))

    def ts(out, a, s1, o1, s2=None, o2=None):
        if o2 is None:
            op("v", [out], [a, s1], lambda: g.vector.tensor_scalar(out[0], a[0], ap(s1), None, o1))
        else:
            op("v", [out], [a, s1, s2], lambda: g.vector.tensor_scalar(out[0], a[0], ap(s1), ap(s2), o1, o2))

    def scan(out, a, b, o1, o2):
        op("v", [out], [a, b], lambda: g.vector.tensor_tensor_scan(out[0], a[0], b[0], 0.0, o1, o2))

    def fill(out, c):
        op("v", [out], [], lambda: g.vector.memset(out[0], c))

    def act(out, a, fn, bias=0.0, scale=1.0):
        op("s", [out], [a, bias, scale], lambda: g.scalar.activation(out[0], a[0], fn, bias=ap(bias), scale=ap(scale)))

    def mms(out, pairs):
        for j, (l, r) in enumerate(pairs):
            op("t", [out], [l, r], lambda: g.tensor.matmul(out[0], l[0], r[0], j == 0, j == len(pairs) - 1))

    def iota(out, pat, base, cm, small=True):
        if small:
            op("g", [out], [], lambda: g.iota(out[0], pat, base, cm, allow_small_or_imprecise_dtypes=True))
        else:
            op("g", [out], [], lambda: g.iota(out[0], pat, base, cm))

    peers = [(me + d) % N for d in range(1, N)]
    plan, off_e, in_e = centre_plan(T, topo, me)
    hs = helpers(T, topo, me)

    def remote(srcs, trs, n, loc):
        rd = regs(srcs)
        order("g", rd, [])
        g.remote_dma_fused(trs, local_sem=T.sem[loc])
        note("d", rd, [], (loc, n, dict(known["g"])))

    def arrives(name, base, width, arr, n):
        note("x", [], [(name, base + o * width, base + (o + 1) * width) for o in peers], (arr, n, {}))

    def col(j):
        return v("cc", j, j + 1)

    def own(reg):
        return v("tb", 2048 * reg + B * me, 2048 * reg + B * me + B) if reg < 5 else v("cf")

    def send_centres(reg):
        s, sem = own(reg), T.sem["ac%d" % reg]
        trs, n = transfers(topo, core, off_e, [T.cores[o] for o in plan[core]], sem, [s[0]] * N, s[0]) if plan[core] else ([], 0)
        total = n + sum(sum(shares(len(off_e), len(plan[h]))) for h in hs)
        if hs:
            more, m = transfers(topo, core, in_e, hs, sem, [s[0]] * N, s[0])
            trs, n = more + trs, n + m
        remote([s], trs, n, "lc%d" % reg)
        arrives("tb", 2048 * reg, B, "ac%d" % reg, total)

    def sel(w, r):
        return v("bz", 144 * w + 15 - r, 144 * w + 143 - r)

    W1024, WM512, WJ, WZ, W1, W256 = range(6)
    ID1, ID256, ID2, IDM, IDM512, IDH = [v("idn", 128 * j, 128 * j + 128) for j in range(6)]
    CP, CPR, CPC, CPC15, CJ, C256, CM512, CPR1, C16, CY, CZ, C8, CS, C15 = [col(4 * j) for j in range(14)]
    ysb = v("sb", YO, YO + B)
    cps, yps, cpp = v("p0", 0, B), v("p0", B, 2 * B), v("p5", B, 2 * B)

    def to_l3(out, terms, more=()):
        pairs = []
        for w, x in terms:
            name, lo = x[1][0][0], x[1][0][1]
            pairs += [(sel(w, r), v(name, lo + r, lo + B, 16)) for r in range(16)]
        mms(out, list(more) + pairs)

    def bzw(w, s):
        act(v("bz", 144 * w, 144 * w + 144), v("bz", 144 * W1, 144 * W1 + 144), F.Identity, 0.0, s)

    def gather_entries(lo, hi):
        act(v("sb", 16 * lo, 16 * hi), ind(v("pool"), v("el", lo, hi)), F.Copy)

    def entry_sums(t, lo, hi):
        for k in range(16):
            tt(v("me", B * k + lo, B * k + hi), v("sb", 16 * lo + k, 16 * hi, 16), v("p0", lo, hi), A.max)
        c = own(t)[1][0]
        pairs = [(v("bo"), v(c[0], c[1] + lo, c[1] + hi))]
        pairs += [(sel(WM512, k), v("sb", 16 * lo + k, 16 * hi, 16)) for k in range(16)]
        pairs += [(sel(W1024, k), v("me", B * k + lo, B * k + hi)) for k in range(16)]
        mms(v("p1", lo, hi), pairs)

    def jump_sum(t):
        b = t % 2
        to_l3(v("p7", 0, 16), [(WJ, v("xw", B * b, B * b + B))])

    def jump(t):
        b = t % 2
        cp(v("s1"), v("p7", 0, 16))
        ts(v("s2"), v("s1"), 255, A.bitwise_and)
        cp(v("jl"), v("s2"))
        tt(v("dy"), ind(v("jm"), v("jl")), v("xw", B * b, B * b + B), A.subtract)

    def prep_s(t):
        act(cps, own(t), F.Copy)
        act(v("cm"), own(t), F.Identity, -1.0)
        act(cpp, own(t), F.Identity, 1.0)
        act(v("sb", 4096 + 15, YO, 16), own(t), F.Copy)
        act(yps, v("dy"), F.Abs)
        act(ysb, v("dy"), F.Abs)

    def stay_key(t):
        tt(v("da"), ysb, cps, A.max)
        to_l3(v("p7", 16, 32), [(WM512, own(t)), (W1024, v("da"))])
        mms(v("p3", B, 2 * B), [(v("bo"), ysb)])

    def stay_key2():
        ts(v("sk"), v("p7", 16, 32), v("sa", 0, 1), A.add)

    def draw():
        ts(v("ui"), v("p3", B, 2 * B), -1.0 / 512, A.mult)
        ts(v("uu"), v("ui"), 63, A.bitwise_and)

    def restart(nn):
        def a():
            act(v("p1", 0, B), v("p1", 0, B), F.Relu, 2047.0, -1.0 / 512)

        def b():
            tt(v("gk"), v("p1", 0, B), nn, A.mult)
            mms(v("p2", B, 2 * B), [(v("bo32"), v("gk"))])
            mms(v("p6", B, 2 * B), [(v("tri"), v("gk"))])

        def c():
            tt(v("up"), v("p2", B, 2 * B), v("uu"), A.mult)
            tt(v("no"), v("p6", B, 2 * B), v("up"), A.is_le)
            to_l3(v("p7", 32, 48), [(WZ, v("no"))], [(ID1, v("zb"))])
        return a, b, c

    def neighbours(t, hooks):
        b = t % 2
        win = v("tb", 2048 * t, 2048 * t + 4096)

        def src(a, z):
            return v("ng", B * a, B * z), ind(win, v("nl", B * b + 16 * a, B * b + 16 * z))
        for a in range(0, 16, 4):
            lo = max(a, VG[t])
            o, w = src(lo, a + 4)
            act(o, w, F.Copy)
            if a == 4:
                for h in hooks.get("s", ()):
                    h()
        if VG[t]:
            cp(*src(0, VG[t]))
        for h in hooks.get(0, ()):
            h()
        for j in range(4):
            a, z = 4 * j, 4 * j + 4
            for k in range(a, z):
                tt(v("mn", B * k, B * k + B), v("ng", B * k, B * k + B), yps, A.max)
            out = v("p%d" % (4 + j % 2), 64 * (j // 2), 64 * (j // 2) + 64)
            pairs = [(ID1, v("iot", 16 * a, 16 * z))]
            pairs += [(sel(WM512, r), v("ng", B * a + r, B * z, 16)) for r in range(16)]
            pairs += [(sel(W1024, r), v("mn", B * a + r, B * z, 16)) for r in range(16)]
            mms(out, pairs)
            if j == 1:
                cp(v("k0"), v("p4", 0, 64))
                tt(v("k0", 0, 16), v("k0", 0, 16), v("sk"), A.min)
            if j == 2:
                tt(v("k1"), v("p5", 0, 64), v("k0"), A.min)
            if j == 3:
                tt(v("k0"), v("p4", 64, 128), v("k1"), A.min)
            for h in hooks.get(j + 1, ()):
                h()

    def decide():
        tt(v("k1"), v("p5", 64, 128), v("k0"), A.min)
        tt(v("k2"), v("k1", 0, 32), v("k1", 32, 64), A.min)
        tt(v("ki"), v("k2", 0, 16), v("k2", 16, 32), A.min)
        ts(v("lo"), v("ki"), 511, A.bitwise_and)

    def stays():
        ts(v("t1"), v("lo"), 256.0, A.is_ge)
        tt(v("t3"), v("t1"), v("yoff"), A.mult)

    def exits_a(t):
        b = t % 2
        cp(v("l1"), v("lo"))
        tt(v("mo"), ind(v("town", 272 * b, 272 * b + 272), v("l1")), v("dg"), A.mult)
        mms(v("p4", 0, B), [(v("bo"), v("mo"))])

    def exits_b(t):
        b = t % 2
        tt(v("mc"), ind(v("tcode", 272 * b, 272 * b + 272), v("l1")), v("dg"), A.mult)
        ts(v("hit"), v("p4", 0, B), CM512, A.is_equal)

    def exits_c():
        mms(v("p3", 0, B), [(v("bo32"), v("mc"))])
        scan(v("cum"), v("hit"), v("hit"), A.add, A.max)
        tt(v("val"), v("hit"), v("cum"), A.mult)
        to_l3(v("p4", B, B + 16), [(W256, v("hit")), (W1, v("val"))])

    def exits_d(t):
        tt(v("pay"), v("p3", 0, B), ysb, A.add)
        ts(v("dl"), v("p4", B, B + 16), -1.0, A.add)
        o, off = iout(v("outw"), v("dl"))
        cp(o, v("pay"), off)
        slot = v("land", 128 * t + 16 * me, 128 * t + 16 * me + 16)
        srcs = [v("outw", B * q, B * q + 16) for q in peers]
        trs, n = transfers(topo, core, off_e[:N - 1], [T.cores[q] for q in peers], T.sem["ax%d" % t], [s[0] for s in srcs], slot[0])
        remote(srcs, trs, n, "lx%d" % t)
        arrives("land", 128 * t, 16, "ax%d" % t, n)
        cp(slot, v("outw", B * me, B * me + 16))

    def count_exits():
        mms(v("p3", 0, 1), [(v("aw"), v("cum", B - 1, B))])
        ts(v("a1", 0, 1), v("p3", 0, 1), -1.0, A.mult, 2048.0, A.add)
        ts(v("a2", 0, 1), v("a1", 0, 1), 63, A.bitwise_and)
        ts(v("sa", 0, 1), v("a2", 0, 1), -512.0, A.mult, -256.0, A.add)

    def prefill():
        for q in range(N):
            dma("y", v("outw", B * q, B * q + 16), v("dum"))

    def move(t, zo):
        b = t % 2
        tt(v("t2"), zo, v("t3"), A.max)
        cp(v("l2"), v("t2"))
        tt(v("c1"), ind(v("sb"), v("l2")), v("cm"), A.max)
        if t + 1 < R:
            act(v("xw", B * b, B * b + B), ind(v("sb"), v("l2")), F.Copy)
        tt(own(t + 2), v("c1"), cpp, A.min)
        if t + 1 == R:
            cp(v("xw", B * b, B * b + B), ind(v("sb"), v("l2")))
        if t + 1 < R:
            send_centres(t + 2)
        if t >= 2:
            dma("y", T.yc[:, B * b:B * b + B], own(t + 2))
            dma("y", T.yx[:, B * b:B * b + B], v("xw", B * b, B * b + B))

    def rows(b):
        lo = 8 + 4096 * b
        return (T.mb[0:128:16, lo:lo + 4096], [("mb", lo, lo + 4096)])

    def receive(t):
        ld = v("land", 128 * t, 128 * t + 128)
        cp(v("yi"), ld)
        tt(v("fr"), ld, v("yi"), A.subtract)
        scan(v("sc"), v("d0"), v("fr"), A.mult, A.max)
        ts(v("rl"), v("sc", 15, 128, 16), CS, A.mult)
        o, off = iout(v("mb"), v("rl"))
        cp(o, v("plc", 128 * t, 128 * t + 128), off)
        nb_ = (t + 1) % 2
        dma("y", v("m2", B * nb_, B * nb_ + B), rows(nb_))
        if t % 2 == 1:
            dma("y", v("m2", B * (1 - nb_), B * (1 - nb_) + B), rows(1 - nb_))
        cp(v("pool", 128 * t, 128 * t + 128), v("yi"))
        if t + 1 < R:
            prefill()
            cp(v("pool", 1024 + 128 * t, 1152 + 128 * t), v("pool", 128 * t, 128 * t + 128))
        if t == 2:
            dma("y", T.yz[:, 0:384], v("pool", 0, 384))
        if t == 3:
            dma("y", T.yz[:, 384:512], v("pool", 384, 512))

    def flux(t):
        b = t % 2
        m = v("m2", B * b, B * b + B)
        if t == 1:
            ts(v("nt", 0, B), m, 1024.0, A.is_ge, 1.0, A.add)
            return v("nt", 0, B)
        if t == 2:
            ts(v("n2"), v("m2"), 1024.0, A.is_ge, 1.0, A.add)
            return v("n2", 0, B)
        ts(v("fl", 0, B), m, 1280.0, A.is_ge)
        tt(v("nt", 0, B), v("fl", 0, B), v("n2", B, 2 * B), A.add)
        return v("nt", 0, B)

    def tables_a(b):
        nm = v("nbi", B * b, B * b + B)
        ts(v("ti"), nm, 255, A.bitwise_and)
        ts(v("ti2"), nm, 8, A.logical_shift_right, 1, A.bitwise_and)
        ts(v("ti3"), nm, 9, A.logical_shift_right)
        cp(v("ib"), v("ti"))
        ts(v("bk"), v("ti2"), 2048.0, A.mult)
        ow = v("town", 272 * b, 272 * b + B)
        cp(ow, v("ti3"))
        mms(v("p4", B, 2 * B), [(ID1, v("ib")), (IDM if b else ID1, v("bk")), (ID256, ow)])
        mms(v("p2", 0, B), [(ID1, v("ib")), (ID2, v("bk")), (ID256, v("kx"))])

    def tables_b(b):
        ts(v("nl", B * b, B * b + B), v("p4", B, 2 * B), 2048.0 * b, A.add)
        act(v("tcode", 272 * b, 272 * b + B), v("p2", 0, B), F.Identity, 8 * 2.0 ** -15, 2.0 ** -15)

    dma("y", own(0), T.cen[:, 0:B])
    dma("s", own(1), T.cen[:, B:2 * B])
    dma("y", v("e2", 0, B), T.ent[:, 0:4096])
    dma("s", v("pool", 0, 1024), T.pl[:])
    dma("y", v("xw"), T.wk[:])
    dma("s", v("jm"), T.jmp[:])
    dma("y", v("pool", 1024, 1536), T.pl[:, 0:512])
    dma("y", v("nbi"), T.nb[:])
    dma("y", v("e2", B, 2 * B), T.ent[:, 4096:8192])
    iota(v("pi", 0, 1), [[0, 1]], 0, 1, False)
    iota(v("iot"), [[1, 256]], 0, 0)
    iota(v("x2"), [[16, 8], [0, 16]], 0, 0)
    iota(v("x3"), [[0, 16], [1, 16]], 0, 0)
    send_centres(0)
    send_centres(1)
    iota(v("kx"), [[2, 8], [-1, 2], [0, 16]], 1, 0)
    ts(v("pj", 0, 1), v("pi", 0, 1), 15, A.bitwise_and)
    cp(CP, v("pi", 0, 1))
    cp(CPR, v("pj", 0, 1))
    tt(CPC, CP, CPR, A.subtract)
    act(CJ, CPR, F.Identity, 1.0, 2.0)
    ts(CPC15, CPC, 15.0, A.add)
    ts(C15, CPR, 15.0, A.is_equal)
    ts(v("bz", 144 * W1, 144 * W1 + 144), v("iot", 0, 144), CPC15, A.is_equal)
    bzw(WJ, CJ)
    bzw(WM512, -512.0)
    bzw(W1024, 1024.0)
    ts(ID1, v("iot", 0, 128), CP, A.is_equal)
    ts(v("bo"), v("x2"), CPC, A.is_equal, -512.0, A.mult)
    ts(v("bo32"), v("x2"), CPC, A.is_equal)
    ts(v("tr0"), v("x2"), CPC, A.is_equal, 64.0, A.mult)
    ts(C8, CPR, 8.0, A.is_equal)
    fill(v("sa", 0, 1), -256.0)
    for m, w in ((ID256, 256.0), (ID2, 2.0), (IDM, -1.0)):
        act(m, ID1, F.Identity, 0.0, w)
    for c, w, a in ((C256, 256.0, 0.0), (CM512, -512.0, 0.0), (CPR1, 1.0, 1.0), (C16, 16.0, 0.0), (CY, 1.0, float(YO))):
        act(c, CPR, F.Identity, a, w)
    act(CZ, C15, F.Identity, 1.0, 4095.0)
    act(CS, C15, F.Identity, 1.0, 32767.0)
    ts(v("dg"), v("x3"), CPR, A.is_equal)
    ts(v("d0"), v("x3", 0, 128), CPR, A.not_equal)
    ts(v("d1"), v("x3", 0, 128), CPR1, A.is_equal, 32767.0, A.mult)
    cp(v("el"), v("e2", 0, B))
    tt(v("d0"), v("d0"), v("d1"), A.add)
    jump_sum(0)
    gather_entries(HCH[0][0], HCH[0][1])
    op("g", [v("tri")], [v("tr0")], lambda: g.affine_select(T.tri[:], T.tr0[:], [[1, 128]], A.is_ge, 0.0, 0, -1))
    iota(v("n2", 0, B), [[0, B]], 1, 0)
    iota(v("sb", 4096, YO), [[0, 4096]], 0, 0)
    iota(v("plc"), [[1, 512]], 1024, 0)
    jump(0)
    jump_sum(1)
    tables_a(0)
    act(cps, own(0), F.Copy)
    for j in range(1, len(HCH[0]) - 1):
        gather_entries(HCH[0][j], HCH[0][j + 1])
    cp(v("m2"), v("e2"))
    for b in range(2):
        dma("y", rows(b), v("m2", B * b, B * b + B))
    dma("y", T.yz[:, 512:1024], v("pool", 512, 1024))
    entry_sums(0, HCH[0][0], HCH[0][1])
    ts(v("nl", 0, B), v("p4", B, 2 * B), 0.0, A.add)
    act(yps, v("dy"), F.Abs)
    act(ysb, v("dy"), F.Abs)
    act(v("tcode", 0, B), v("p2", 0, B), F.Identity, 8 * 2.0 ** -15, 2.0 ** -15)
    bzw(WZ, CZ)
    act(v("zb"), v("iot", 0, 16), F.Identity, C16, 256.0)
    tables_a(1)
    for j in range(1, len(HCH[0]) - 1):
        entry_sums(0, HCH[0][j], HCH[0][j + 1])
    tables_b(1)
    stay_key(0)
    r0 = restart(v("n2", 0, B))

    def late():
        act(v("cm"), own(0), F.Identity, -1.0)
        act(v("sb", 4096 + 15, YO, 16), own(0), F.Copy)
        act(v("yoff"), v("iot", 0, 16), F.Identity, CY, 16.0)
        act(v("dum"), v("iot", 0, 16), F.Identity, (8200.0 + 16 * me) * 2.0 ** -15, 2.0 ** -15)
        prefill()
        bzw(W256, C256)
        act(v("aw"), v("iot", 0, 128), F.Identity, C8, 0.0)
        for b in range(2):
            act(v("town", 272 * b + B, 272 * b + 272), v("iot", 0, 16), F.Identity, 8.0, 0.0)
            act(v("tcode", 272 * b + B, 272 * b + 272), v("iot", 0, 16), F.Identity, 0.0, 0.0)
        act(IDM512, ID1, F.Identity, 0.0, -512.0)
        act(v("id32"), ID1, F.Copy)

    for t in range(R):
        b, last = t % 2, t == R - 1
        if t == 0:
            act(cpp, own(0), F.Identity, 1.0)
            neighbours(0, {"s": [r0[0]], 1: [draw, stay_key2, r0[1]], 2: [r0[2]], 3: [late], 4: [lambda: cp(v("zo"), v("p7", 32, 48))]})
            jump(1)
            decide()
            stays()
            move(0, v("zo"))
            exits_a(0)
            exits_b(0)
            exits_c()
            exits_d(0)
        else:
            ch = HCH[1]
            hooks = {j: [] for j in range(5)}
            hooks[RECV_AT].append(lambda: receive(t - 1))
            hooks[LIST_AT].append(lambda: cp(v("el"), v("m2", B * b, B * b + B)))
            neighbours(t, hooks)
            for j in range(len(ch) - 1):
                gather_entries(max(ch[j], HV[t]), ch[j + 1])
            decide()
            if last:
                exits_a(t)
                stays()
                exits_b(t)
                exits_c()
                exits_d(t)
            else:
                stays()
                jump_sum(t + 1)
            if HV[t]:
                cp(v("sb", 0, 16 * HV[t]), ind(v("pool"), v("el", 0, HV[t])))
            nn = flux(t)
            for j in range(len(ch) - 1):
                entry_sums(t, ch[j], ch[j + 1])
            ra, rb, rc = restart(nn)
            ra()
            if last:
                steps = [rb, rc, lambda: move(t, v("p7", 32, 48))]
                steps.insert(TAIL, lambda: receive(t))
                for s in steps:
                    s()
            else:
                exits_a(t)
                rb()
                exits_b(t)
                rc()
                exits_c()
                move(t, v("p7", 32, 48))
                exits_d(t)
        if not last:
            if t:
                jump(t + 1)
            prep_s(t + 1)
            count_exits()
            stay_key(t + 1)
            draw()
            stay_key2()
    act(v("sg"), v("m2"), F.Sign, -1023.5)
    mms(v("p1"), [(v("id32"), v("m2")), (IDM512, v("sg"))])
    ts(v("fl"), v("m2"), 1280.0, A.is_ge)
    act(v("ef"), v("p1"), F.Identity, -512.0)
    for b in range(2):
        dma("s", T.ye[:, 4096 * b:4096 * b + 4096], v("ef", B * b, B * b + B))
        tt(v("nt", B * b, B * b + B), v("fl", B * b, B * b + B), v("n2", B * b, B * b + B), A.add)
        dma("y", T.yn[:, 4096 * b:4096 * b + 4096], v("nt", B * b, B * b + B))
    for sem, val in final.items():
        if all(known[q].get(sem, 0) < val for q in eng):
            g.sync.wait_ge(T.sem[sem], val)
